import numpy as np
import ml_dtypes


def mxq(x, axis, fmt="e4m3"):
    dtype, down = {"e4m3": (ml_dtypes.float8_e4m3fn, 7), "e5m2": (ml_dtypes.float8_e5m2, 14)}[fmt]
    v = np.moveaxis(np.asarray(x, np.float32).astype(ml_dtypes.bfloat16).astype(np.float64), axis, -1)
    blocks = v.reshape(v.shape[:-1] + (-1, 32))
    amax = np.abs(blocks).max(-1, keepdims=True)
    byte = np.maximum(np.where(amax > 0, np.frexp(amax)[1] - 1 + 127, 0) - down, 1)
    scale = np.exp2(byte - 127.0)
    codes = (blocks / scale).astype(np.float32).astype(dtype).astype(np.float64)
    return np.moveaxis((codes * scale).reshape(v.shape), -1, axis)


WIDE = False


def mx_kscale(k):
    if not WIDE:
        return np.ones(k)
    levels = np.array([18, -18])
    if k % 512:
        return np.exp2(np.random.permutation(np.resize(levels, k // 32))).repeat(32)
    a = np.empty((k // 512, 16))
    for p in range(k // 512):
        a[p, :8] = np.random.permutation(np.resize(levels, 8))
        for g in range(8):
            far = levels[np.abs(levels - a[p, g]) >= 10]
            a[p, g + 8] = far[np.random.randint(len(far))]
    return np.exp2(a.ravel()).repeat(32)


def f64(x):
    return np.asarray(x).astype(np.float64)


def striped(idx):
    return np.tile(np.asarray(idx).reshape(-1, 16).T, (8, 1)).astype(np.uint16)


def unstriped(offs):
    return offs[:16].T.reshape(-1).astype(np.int64)


V, K, E, D, DV = 1024, 2, 2048, 256, 512


def setup_inputs():
    n = np.random.standard_normal
    v = mx_kscale(DV)[:, None]
    coarse = lambda x: x.astype(np.float32).astype(ml_dtypes.bfloat16).astype(np.float64)
    return {
        "dyT": (coarse(n((DV, V))) * v).astype(np.float32),
        "hE": (np.random.randint(1, 32, (DV, E)) / 32.0).astype(np.float32),
        "ew": np.tile(np.random.randint(8, 33, E) / 16.0, (128, 1)).astype(np.float32),
        "wm": (n((DV, D)) / np.sqrt(DV) / v).astype(np.float32),
        "offs": striped(np.random.randint(0, V, E)),
        "offs2": striped(np.random.permutation(E)),
    }


def reference(dyT, hE, ew, wm, offs, offs2):
    h = f64(hE)
    dz = f64(ew)[:1] * f64(dyT)[:, unstriped(offs)] * h * (1.0 - h)
    dm = mxq(f64(wm), 0, "e4m3").T @ mxq(dz, 0, "e5m2")
    return dm[:, unstriped(offs2)].reshape(D, V, K).sum(-1)

@@ -1,0 +1,217 @@
+from contextlib import ExitStack
+
+import concourse.mybir as mybir
+from concourse.masks import make_identity
+
+V, E, D, DV = 1024, 2048, 256, 512
+FLOPS = 2 * DV * D * E
+
+F32 = mybir.dt.float32
+BF16 = mybir.dt.bfloat16
+U32 = mybir.dt.uint32
+U16 = mybir.dt.uint16
+U8 = mybir.dt.uint8
+E4M3 = mybir.dt.float8_e4m3fn_x4
+E5M2 = mybir.dt.float8_e5m2_x4
+ACT = mybir.ActivationFunctionType
+ALU = mybir.AluOpType
+
+P = 128
+PACK = 4
+N_MM = 512
+PIECES = [[512,512,512,512],[512,512,512,256,256]]
+LAST_V = 1
+
+
+def tile_attend_gmp_sig_ew_kernel(tc, dyT, hE, ew, wm, offs, offs2, out):
+    nc = tc.nc
+    with ExitStack() as ctx:
+        keep = ctx.enter_context(tc.tile_pool(name="keep", bufs=1))
+        ring = ctx.enter_context(tc.tile_pool(name="ring", bufs=4))
+        ps_fwd = ctx.enter_context(tc.psum_pool(name="ps_fwd", bufs=3))
+        ps_back = ctx.enter_context(tc.psum_pool(name="ps_back", bufs=2))
+        ps_mm = ctx.enter_context(tc.psum_pool(name="ps_mm", bufs=3))
+
+        dst_list = keep.tile([P, E // 16], U16, name="dst_list")
+        src_list = keep.tile([P, E // 16], U16, name="src_list")
+        dy = [keep.tile([P, V], F32, name=f"dy{t}") for t in range(PACK)]
+        h = keep.tile([P, PACK, E], F32, name="h")
+        g = keep.tile([P, PACK, E], F32, name="g")
+        ew_all = keep.tile([P, E], F32, name="ew_all")
+        ew_rows = keep.tile([P, P], F32, name="ew_rows")
+        ew_cols = keep.tile([P, E // P], F32, name="ew_cols")
+        ident = keep.tile([P, P], F32, name="ident")
+        w_raw = keep.tile([P, PACK, D], F32, name="w_raw")
+        w_bf = keep.tile([P, D * PACK], BF16, name="w_bf", align_bytes=64)
+        w_codes = keep.tile([P, D], U32, name="w_codes", align_bytes=64)
+        w_scales = keep.tile([P, D], U8, name="w_scales", align_bytes=64)
+        dz_bf = keep.tile([P, E * PACK], BF16, name="dz_bf", align_bytes=64)
+        dz_codes = keep.tile([P, E], U32, name="dz_codes", align_bytes=64)
+        dz_scales = keep.tile([P, E], U8, name="dz_scales", align_bytes=64)
+        dm = [keep.tile([P, E], F32, name=f"dm{b}") for b in range(D // P)]
+        picked = [keep.tile([P, E], F32, name=f"picked{b}") for b in range(D // P)]
+        res = [keep.tile([P, V], F32, name=f"res{b}") for b in range(D // P)]
+        warm = keep.tile([P, 8], F32, name="warm")
+        probe = keep.tile([P, 64], F32, name="probe")
+
+        dy_planes = dyT.rearrange("(p t) v -> p t v", t=PACK)
+        h_planes = hE.rearrange("(p t) e -> p t e", t=PACK)
+
+        def warm_up():
+            nc.vector.memset(warm[:], 0.0)
+            nc.scalar.activation(out=warm[:, 0:1], in_=warm[:, 1:2], func=ACT.Square, bias=-0.5)
+
+        def ld_dy(t):
+            nc.sync.dma_start(dy[t][:], dy_planes[:, t, :])
+
+        def ld_h(e0, n, t0, t1):
+            nc.sync.dma_start(h[:, t0:t1, e0 : e0 + n], h_planes[:, t0:t1, e0 : e0 + n])
+
+        def ld_ew(e0, n):
+            nc.sync.dma_start(ew_all[:, e0 : e0 + n], ew[:, e0 : e0 + n])
+
+        def ld_ewr():
+            nc.sync.dma_start(ew_rows[:], ew[0:8, :].rearrange("a (r c) -> (a r) c", c=P))
+
+        def ld_w():
+            nc.sync.dma_start(w_raw[:], wm.rearrange("(p t) d -> p t d", t=PACK))
+
+        def ld_l1():
+            nc.sync.dma_start(dst_list[:], offs)
+
+        def ld_l2():
+            nc.sync.dma_start(src_list[:], offs2)
+
+        def sq(e0, n, t0, t1):
+            x = h[:, t0:t1, e0 : e0 + n]
+            nc.scalar.activation(out=x, in_=x, func=ACT.Square, bias=-0.5)
+
+        def aff(e0, n, t0, t1, on_vector):
+            x = h[:, t0:t1, e0 : e0 + n]
+            if on_vector:
+                nc.vector.tensor_scalar(x, x, 1.0, -0.25, ALU.mult, ALU.add)
+            else:
+                nc.scalar.activation(out=x, in_=x, func=ACT.Copy, scale=1.0, bias=-0.25)
+
+        def gather(e0, n, t, by_ew):
+            lst = dst_list[:, e0 // 16 : (e0 + n) // 16]
+            other = ew_all[:, e0 : e0 + n] if by_ew else h[:, t, e0 : e0 + n]
+            nc.vector.tensor_tensor(g[:, t, e0 : e0 + n], dy[t][:].indirect(lst), other, ALU.mult)
+
+        turned = {}
+
+        def weigh(b):
+            bank = ps_fwd.tile([P, PACK, P], F32, name="fwd")
+            for t in range(PACK):
+                nc.tensor.transpose(bank[:, t, :], g[:, t, b * P : (b + 1) * P], ident[:])
+            dzt = ring.tile([P, 2, P, 2], BF16, name="dzt")
+            nc.scalar.activation(out=dzt[:], in_=bank[:].rearrange("e (u i) p -> e u p i", i=2), func=ACT.Copy,
+                                 scale=ew_cols[:, b : b + 1])
+            turned[b] = dzt
+
+        def turn_back(pair, on_vector):
+            bank = ps_back.tile([P, 2, 2 * P], F32, name="back")
+            for k in range(2):
+                words = turned[2 * pair + k][:].rearrange("e u p i -> e (u p i)").bitcast(F32)
+                for u in range(2):
+                    nc.tensor.transpose(bank[:, u, k * P : (k + 1) * P], words[:, u * P : (u + 1) * P], ident[:])
+            dst = dz_bf[:, pair * 2 * P * PACK : (pair + 1) * 2 * P * PACK].bitcast(F32).rearrange("p (e u) -> p e u", u=2)
+            if on_vector:
+                nc.vector.tensor_copy(dst, bank[:].rearrange("p u e -> p e u"))
+            else:
+                nc.scalar.copy(dst, bank[:].rearrange("p u e -> p e u"))
+
+        def direct(e0, n):
+            dst = dz_bf[:, e0 * PACK : (e0 + n) * PACK].rearrange("p (e t) -> p e t", t=PACK)
+            nc.vector.scalar_tensor_tensor(
+                dst, h[:, :, e0 : e0 + n].rearrange("p t e -> p e t"), 0.25,
+                g[:, :, e0 : e0 + n].rearrange("p t e -> p e t"), ALU.subtract, ALU.mult)
+
+        def quantize(e0, n):
+            nc.vector.quantize_mx(out=dz_codes[:, e0 : e0 + n].bitcast(E5M2), scales=dz_scales[:, e0 : e0 + n],
+                                  in_=dz_bf[:, e0 * PACK : (e0 + n) * PACK])
+
+        def multiply(c, v0, v1):
+            cols = slice(c * N_MM, (c + 1) * N_MM)
+            for b in range(D // P):
+                acc = ps_mm.tile([P, N_MM], F32, name="acc")
+                nc.tensor.matmul_mx(out=acc[:], lhsT=w_codes[:, b * P : (b + 1) * P].bitcast(E4M3),
+                                    lhsT_scale=w_scales[:, b * P : (b + 1) * P],
+                                    rhs=dz_codes[:, cols].bitcast(E5M2), rhs_scale=dz_scales[:, cols],
+                                    start=True, stop=True)
+                if (v0, v1)[b]:
+                    nc.vector.tensor_scalar(dm[b][:, cols], acc[:], -1.0, None, ALU.mult)
+                else:
+                    nc.scalar.activation(out=dm[b][:, cols], in_=acc[:], func=ACT.Copy, scale=-1.0)
+
+        def weights(on_vector):
+            src = w_raw[:].rearrange("p t d -> p d t")
+            dst = w_bf[:].rearrange("p (d t) -> p d t", t=PACK)
+            if on_vector:
+                nc.vector.tensor_copy(dst, src)
+            else:
+                nc.scalar.copy(dst, src)
+
+        def weights_q():
+            nc.vector.quantize_mx(out=w_codes[:].bitcast(E4M3), scales=w_scales[:], in_=w_bf[:])
+
+        def edge_weights():
+            make_identity(nc, ident[:])
+            bank = ps_mm.tile([P, N_MM], F32, name="acc")
+            nc.tensor.transpose(bank[:, 0:P], ew_rows[:], ident[:])
+            nc.scalar.copy(ew_cols[:], bank[:, 0 : E // P])
+
+        warm_up()
+        ld_dy(0)
+        ld_l1()
+        ld_ew(0, 512)
+        for t in range(1, 4):
+            ld_dy(t)
+        ld_ew(512, 512)
+        ld_h(0, 512, 0, 4)
+        ld_ew(1024, 1024)
+        ld_w()
+        for c in range(1, 4):
+            ld_h(512 * c, 512, 0, 4)
+        ld_l2()
+        for c in range(2):
+            for t in range(4):
+                gather(512 * c, 512, t, True)
+        for c in range(4):
+            sq(512 * c, 512, 0, 2)
+            sq(512 * c, 512, 2, 4)
+            if c == 0:
+                weights(False)
+        direct(0, 512)
+        gather(1024, 512, 0, True)
+        weights_q()
+        quantize(0, 512)
+        multiply(0, 0, 0)
+        for t in range(1, 4):
+            gather(1024, 512, t, True)
+        direct(512, 512)
+        gather(1536, 512, 0, True)
+        quantize(512, 512)
+        multiply(1, 0, 0)
+        for t in range(1, 4):
+            gather(1536, 512, t, True)
+        direct(1024, 512)
+        direct(1536, 256)
+        quantize(1024, 512)
+        multiply(2, 0, 0)
+        direct(1792, 128)
+        quantize(1536, 256)
+        direct(1920, 128)
+        quantize(1792, 128)
+        quantize(1920, 128)
+        multiply(3, 1, 0)
+
+        for b in range(D // P):
+            lo = 0
+            for j, n in enumerate(PIECES[b]):
+                nc.vector.tensor_copy(picked[b][:, lo : lo + n], dm[b][:].indirect(src_list[:, lo // 16 : (lo + n) // 16]))
+                xs = slice(lo // 2, (lo + n) // 2)
+                eng = nc.vector if (b == 1 and j >= len(PIECES[b]) - LAST_V) else nc.gpsimd
+                eng.tensor_tensor(res[b][:, xs], picked[b][:, lo : lo + n : 2], picked[b][:, lo + 1 : lo + n : 2], ALU.add)
+                nc.sync.dma_start(out[b * P : (b + 1) * P, xs], res[b][:, xs])
+                lo += n

@@ -35,9 +35,11 @@ def tile_attend_gmp_sig_ew_kernel(tc, dyT, hE, ew, wm, offs, offs2, out):
         dst_list = keep.tile([P, E // 16], U16, name="dst_list")
         src_list = keep.tile([P, E // 16], U16, name="src_list")
         dy = [keep.tile([P, V], F32, name=f"dy{t}") for t in range(PACK)]
-        h = keep.tile([P, PACK, E], F32, name="h")
-        g = keep.tile([P, PACK, E], F32, name="g")
-        ew_all = keep.tile([P, E], F32, name="ew_all")
+        CH = 512
+        hs, ews = {}, {}
+        gt = {(c, t): keep.tile([P, CH], F32, name=f"gt{c}{t}") for c in range(2) for t in range(PACK)}
+        gd = {c: keep.tile([P, PACK, CH], F32, name=f"gd{c}") for c in (2, 3)}
+        qd = {c: keep.tile([P, PACK, CH], F32, name=f"qd{c}") for c in (2, 3)}
         ew_rows = keep.tile([P, P], F32, name="ew_rows")
         ew_cols = keep.tile([P, E // P], F32, name="ew_cols")
         ident = keep.tile([P, P], F32, name="ident")
@@ -45,12 +47,10 @@ def tile_attend_gmp_sig_ew_kernel(tc, dyT, hE, ew, wm, offs, offs2, out):
         w_bf = keep.tile([P, D * PACK], BF16, name="w_bf", align_bytes=64)
         w_codes = keep.tile([P, D], U32, name="w_codes", align_bytes=64)
         w_scales = keep.tile([P, D], U8, name="w_scales", align_bytes=64)
-        dz_bf = keep.tile([P, E * PACK], BF16, name="dz_bf", align_bytes=64)
-        dz_codes = keep.tile([P, E], U32, name="dz_codes", align_bytes=64)
-        dz_scales = keep.tile([P, E], U8, name="dz_scales", align_bytes=64)
+        dz_bf = [keep.tile([P, CH * PACK], BF16, name=f"dz_bf{c}", align_bytes=64) for c in range(4)]
+        dz_codes = [keep.tile([P, CH], U32, name=f"dz_codes{c}", align_bytes=64) for c in range(4)]
+        dz_scales = [keep.tile([P, CH], U8, name=f"dz_scales{c}", align_bytes=64) for c in range(4)]
         dm = [keep.tile([P, E], F32, name=f"dm{b}") for b in range(D // P)]
-        picked = [keep.tile([P, E], F32, name=f"picked{b}") for b in range(D // P)]
-        res = [keep.tile([P, V], F32, name=f"res{b}") for b in range(D // P)]
         warm = keep.tile([P, 8], F32, name="warm")
         probe = keep.tile([P, 64], F32, name="probe")
 
@@ -65,10 +65,12 @@ def tile_attend_gmp_sig_ew_kernel(tc, dyT, hE, ew, wm, offs, offs2, out):
             nc.sync.dma_start(dy[t][:], dy_planes[:, t, :])
 
         def ld_h(e0, n, t0, t1):
-            nc.sync.dma_start(h[:, t0:t1, e0 : e0 + n], h_planes[:, t0:t1, e0 : e0 + n])
+            hs[e0, t0] = keep.tile([P, t1 - t0, n], F32, name=f"h{e0}_{t0}")
+            nc.sync.dma_start(hs[e0, t0][:], h_planes[:, t0:t1, e0 : e0 + n])
 
         def ld_ew(e0, n):
-            nc.sync.dma_start(ew_all[:, e0 : e0 + n], ew[:, e0 : e0 + n])
+            ews[e0] = keep.tile([P, n], F32, name=f"ew{e0}")
+            nc.sync.dma_start(ews[e0][:], ew[:, e0 : e0 + n])
 
         def ld_ewr():
             nc.sync.dma_start(ew_rows[:], ew[0:8, :].rearrange("a (r c) -> (a r) c", c=P))
@@ -83,11 +85,12 @@ def tile_attend_gmp_sig_ew_kernel(tc, dyT, hE, ew, wm, offs, offs2, out):
             nc.sync.dma_start(src_list[:], offs2)
 
         def sq(e0, n, t0, t1):
-            x = h[:, t0:t1, e0 : e0 + n]
-            nc.scalar.activation(out=x, in_=x, func=ACT.Square, bias=-0.5)
+            x = hs[e0, t0][:]
+            y = x if e0 < 1024 else qd[e0 // CH][:, t0:t1, :]
+            nc.scalar.activation(out=y, in_=x, func=ACT.Square, bias=-0.5)
 
         def aff(e0, n, t0, t1, on_vector):
-            x = h[:, t0:t1, e0 : e0 + n]
+            x = hs[e0, t0][:]
             if on_vector:
                 nc.vector.tensor_scalar(x, x, 1.0, -0.25, ALU.mult, ALU.add)
             else:
@@ -95,54 +98,62 @@ def tile_attend_gmp_sig_ew_kernel(tc, dyT, hE, ew, wm, offs, offs2, out):
 
         def gather(e0, n, t, by_ew):
             lst = dst_list[:, e0 // 16 : (e0 + n) // 16]
-            other = ew_all[:, e0 : e0 + n] if by_ew else h[:, t, e0 : e0 + n]
-            nc.vector.tensor_tensor(g[:, t, e0 : e0 + n], dy[t][:].indirect(lst), other, ALU.mult)
+            other = ews[e0][:] if by_ew else hs[e0, t][:, 0, :]
+            nc.vector.tensor_tensor(gd[e0 // CH][:, t, :] if by_ew else gt[e0 // CH, t][:], dy[t][:].indirect(lst), other, ALU.mult)
 
-        turned = {}
+        turned, fwd, backs, accs, ew_bank = {}, {}, {}, {}, {}
+
+        def turn(b):
+            fwd[b] = ps_fwd.tile([P, PACK, P], F32, name="fwd")
+            for t in range(PACK):
+                nc.tensor.transpose(fwd[b][:, t, :], gt[b // 4, t][:, (b % 4) * P : (b % 4 + 1) * P], ident[:])
 
         def weigh(b):
-            bank = ps_fwd.tile([P, PACK, P], F32, name="fwd")
-            for t in range(PACK):
-                nc.tensor.transpose(bank[:, t, :], g[:, t, b * P : (b + 1) * P], ident[:])
-            dzt = ring.tile([P, 2, P, 2], BF16, name="dzt")
-            nc.scalar.activation(out=dzt[:], in_=bank[:].rearrange("e (u i) p -> e u p i", i=2), func=ACT.Copy,
+            turned[b] = ring.tile([P, 2, P, 2], BF16, name="dzt")
+            nc.scalar.activation(out=turned[b][:], in_=fwd[b][:].rearrange("e (u i) p -> e u p i", i=2), func=ACT.Copy,
                                  scale=ew_cols[:, b : b + 1])
-            turned[b] = dzt
 
-        def turn_back(pair, on_vector):
-            bank = ps_back.tile([P, 2, 2 * P], F32, name="back")
-            for k in range(2):
-                words = turned[2 * pair + k][:].rearrange("e u p i -> e (u p i)").bitcast(F32)
-                for u in range(2):
-                    nc.tensor.transpose(bank[:, u, k * P : (k + 1) * P], words[:, u * P : (u + 1) * P], ident[:])
-            dst = dz_bf[:, pair * 2 * P * PACK : (pair + 1) * 2 * P * PACK].bitcast(F32).rearrange("p (e u) -> p e u", u=2)
+        def back(b):
+            pair, k = divmod(b, 2)
+            if pair not in backs:
+                backs[pair] = ps_back.tile([P, 2, 2 * P], F32, name="back")
+            words = turned[b][:].rearrange("e u p i -> e (u p i)").bitcast(F32)
+            for u in range(2):
+                nc.tensor.transpose(backs[pair][:, u, k * P : (k + 1) * P], words[:, u * P : (u + 1) * P], ident[:])
+
+        def unload(pair, on_vector):
+            dst = dz_bf[pair // 2][:, (pair % 2) * 2 * P * PACK : (pair % 2 + 1) * 2 * P * PACK].bitcast(F32).rearrange("p (e u) -> p e u", u=2)
             if on_vector:
-                nc.vector.tensor_copy(dst, bank[:].rearrange("p u e -> p e u"))
+                nc.vector.tensor_copy(dst, backs[pair][:].rearrange("p u e -> p e u"))
             else:
-                nc.scalar.copy(dst, bank[:].rearrange("p u e -> p e u"))
+                nc.scalar.copy(dst, backs[pair][:].rearrange("p u e -> p e u"))
 
         def direct(e0, n):
-            dst = dz_bf[:, e0 * PACK : (e0 + n) * PACK].rearrange("p (e t) -> p e t", t=PACK)
+            c, e0 = divmod(e0, CH)
+            dst = dz_bf[c][:, e0 * PACK : (e0 + n) * PACK].rearrange("p (e t) -> p e t", t=PACK)
             nc.vector.scalar_tensor_tensor(
-                dst, h[:, :, e0 : e0 + n].rearrange("p t e -> p e t"), 0.25,
-                g[:, :, e0 : e0 + n].rearrange("p t e -> p e t"), ALU.subtract, ALU.mult)
+                dst, qd[c][:, :, e0 : e0 + n].rearrange("p t e -> p e t"), 0.25,
+                gd[c][:, :, e0 : e0 + n].rearrange("p t e -> p e t"), ALU.subtract, ALU.mult)
 
         def quantize(e0, n):
-            nc.vector.quantize_mx(out=dz_codes[:, e0 : e0 + n].bitcast(E5M2), scales=dz_scales[:, e0 : e0 + n],
-                                  in_=dz_bf[:, e0 * PACK : (e0 + n) * PACK])
+            c, e0 = divmod(e0, CH)
+            nc.vector.quantize_mx(out=dz_codes[c][:, e0 : e0 + n].bitcast(E5M2), scales=dz_scales[c][:, e0 : e0 + n],
+                                  in_=dz_bf[c][:, e0 * PACK : (e0 + n) * PACK])
 
-        def multiply(c, v0, v1):
+        def multiply(c, b):
             cols = slice(c * N_MM, (c + 1) * N_MM)
-            for b in range(D // P):
-                acc = ps_mm.tile([P, N_MM], F32, name="acc")
-                nc.tensor.matmul_mx(out=acc[:], lhsT=w_codes[:, b * P : (b + 1) * P].bitcast(E4M3),
-                                    lhsT_scale=w_scales[:, b * P : (b + 1) * P],
-                                    rhs=dz_codes[:, cols].bitcast(E5M2), rhs_scale=dz_scales[:, cols],
-                                    start=True, stop=True)
-                if (v0, v1)[b]:
-                    nc.vector.tensor_scalar(dm[b][:, cols], acc[:], -1.0, None, ALU.mult)
-                else:
-                    nc.scalar.activation(out=dm[b][:, cols], in_=acc[:], func=ACT.Copy, scale=-1.0)
+            accs[c, b] = ps_mm.tile([P, N_MM], F32, name="acc")
+            nc.tensor.matmul_mx(out=accs[c, b][:], lhsT=w_codes[:, b * P : (b + 1) * P].bitcast(E4M3),
+                                lhsT_scale=w_scales[:, b * P : (b + 1) * P],
+                                rhs=dz_codes[c][:].bitcast(E5M2), rhs_scale=dz_scales[c][:],
+                                start=True, stop=True)
+
+        def evac(c, b, on_vector):
+            cols = slice(c * N_MM, (c + 1) * N_MM)
+            if on_vector:
+                nc.vector.tensor_scalar(dm[b][:, cols], accs[c, b][:], -1.0, None, ALU.mult)
+            else:
+                nc.scalar.activation(out=dm[b][:, cols], in_=accs[c, b][:], func=ACT.Copy, scale=-1.0)
 
         def weights(on_vector):
             src = w_raw[:].rearrange("p t d -> p d t")
@@ -155,63 +166,138 @@ def tile_attend_gmp_sig_ew_kernel(tc, dyT, hE, ew, wm, offs, offs2, out):
         def weights_q():
             nc.vector.quantize_mx(out=w_codes[:].bitcast(E4M3), scales=w_scales[:], in_=w_bf[:])
 
-        def edge_weights():
+        def ew_turn():
             make_identity(nc, ident[:])
-            bank = ps_mm.tile([P, N_MM], F32, name="acc")
-            nc.tensor.transpose(bank[:, 0:P], ew_rows[:], ident[:])
-            nc.scalar.copy(ew_cols[:], bank[:, 0 : E // P])
+            ew_bank[0] = ps_mm.tile([P, N_MM], F32, name="acc")
+            nc.tensor.transpose(ew_bank[0][:, 0:P], ew_rows[:], ident[:])
+
+        def ew_copy():
+            nc.scalar.copy(ew_cols[:], ew_bank[0][:, 0 : E // P])
 
         warm_up()
+        ld_h(0, 512, 0, 1)
         ld_dy(0)
         ld_l1()
-        ld_ew(0, 512)
-        for t in range(1, 4):
-            ld_dy(t)
-        ld_ew(512, 512)
-        ld_h(0, 512, 0, 4)
-        ld_ew(1024, 1024)
+        ld_ew(1024, 512)
+        ld_h(0, 512, 1, 2)
+        ld_dy(1)
+        ld_h(512, 512, 0, 1)
+        ld_h(0, 512, 2, 3)
+        ld_dy(2)
+        ld_h(512, 512, 1, 2)
+        ld_h(0, 512, 3, 4)
+        ld_dy(3)
+        ld_ewr()
+        ld_h(512, 512, 2, 3)
+        ld_h(512, 512, 3, 4)
+        ld_h(1024, 512, 0, 2)
+        ld_h(1024, 512, 2, 4)
+        ld_ew(1536, 512)
         ld_w()
-        for c in range(1, 4):
-            ld_h(512 * c, 512, 0, 4)
+        ld_h(1536, 512, 0, 2)
+        ld_h(1536, 512, 2, 4)
         ld_l2()
-        for c in range(2):
-            for t in range(4):
-                gather(512 * c, 512, t, True)
-        for c in range(4):
-            sq(512 * c, 512, 0, 2)
-            sq(512 * c, 512, 2, 4)
-            if c == 0:
-                weights(False)
-        direct(0, 512)
-        gather(1024, 512, 0, True)
+        sq(0, 512, 0, 1)
+        aff(0, 512, 0, 1, 1)
+        gather(0, 512, 0, 0)
+        gather(1024, 512, 0, 1)
+        sq(0, 512, 1, 2)
+        aff(0, 512, 1, 2, 0)
+        gather(0, 512, 1, 0)
+        sq(512, 512, 0, 1)
+        sq(0, 512, 2, 3)
+        gather(1024, 512, 1, 1)
+        aff(0, 512, 2, 3, 0)
+        aff(512, 512, 0, 1, 0)
+        gather(0, 512, 2, 0)
+        sq(512, 512, 1, 2)
+        sq(0, 512, 3, 4)
+        gather(1024, 512, 2, 1)
+        aff(0, 512, 3, 4, 0)
+        ew_turn()
+        aff(512, 512, 1, 2, 0)
+        gather(0, 512, 3, 0)
+        ew_copy()
+        sq(512, 512, 2, 3)
+        sq(512, 512, 3, 4)
+        gather(1024, 512, 3, 1)
+        turn(0)
+        aff(512, 512, 2, 3, 0)
+        aff(512, 512, 3, 4, 0)
+        turn(1)
+        gather(512, 512, 0, 0)
+        weigh(0)
+        turn(2)
+        sq(1024, 512, 0, 2)
+        gather(512, 512, 1, 0)
+        back(0)
+        turn(3)
+        weigh(1)
+        gather(512, 512, 2, 0)
+        sq(1024, 512, 2, 4)
+        back(1)
+        gather(512, 512, 3, 0)
+        weigh(2)
+        weigh(3)
+        direct(1024, 256)
+        back(2)
+        unload(0, 0)
+        back(3)
+        weights(0)
+        turn(4)
+        gather(1536, 512, 0, 1)
+        turn(5)
+        unload(1, 0)
+        turn(6)
+        direct(1280, 256)
+        weigh(4)
+        sq(1536, 512, 0, 2)
+        back(4)
+        gather(1536, 512, 1, 1)
+        turn(7)
+        weigh(5)
         weights_q()
-        quantize(0, 512)
-        multiply(0, 0, 0)
-        for t in range(1, 4):
-            gather(1024, 512, t, True)
-        direct(512, 512)
-        gather(1536, 512, 0, True)
-        quantize(512, 512)
-        multiply(1, 0, 0)
-        for t in range(1, 4):
-            gather(1536, 512, t, True)
-        direct(1024, 512)
-        direct(1536, 256)
+        sq(1536, 512, 2, 4)
+        back(5)
+        gather(1536, 512, 2, 1)
+        weigh(6)
         quantize(1024, 512)
-        multiply(2, 0, 0)
-        direct(1792, 128)
+        weigh(7)
+        gather(1536, 512, 3, 1)
+        unload(2, 0)
+        multiply(2, 0)
+        back(6)
+        evac(2, 0, 0)
+        quantize(0, 512)
+        back(7)
+        direct(1536, 256)
+        unload(3, 0)
+        multiply(0, 0)
+        evac(0, 0, 0)
+        quantize(512, 512)
+        direct(1792, 256)
+        multiply(1, 0)
+        evac(1, 0, 0)
         quantize(1536, 256)
-        direct(1920, 128)
-        quantize(1792, 128)
-        quantize(1920, 128)
-        multiply(3, 1, 0)
+        quantize(1792, 256)
+        multiply(3, 0)
+        multiply(2, 1)
+        evac(3, 0, 1)
+        multiply(0, 1)
+        evac(2, 1, 0)
+        multiply(1, 1)
+        evac(0, 1, 0)
+        multiply(3, 1)
+        evac(1, 1, 0)
+        evac(3, 1, 0)
 
         for b in range(D // P):
             lo = 0
             for j, n in enumerate(PIECES[b]):
-                nc.vector.tensor_copy(picked[b][:, lo : lo + n], dm[b][:].indirect(src_list[:, lo // 16 : (lo + n) // 16]))
-                xs = slice(lo // 2, (lo + n) // 2)
+                picked = keep.tile([P, n], F32, name=f"picked{b}{j}")
+                res = keep.tile([P, n // 2], F32, name=f"res{b}{j}")
+                nc.vector.tensor_copy(picked[:], dm[b][:].indirect(src_list[:, lo // 16 : (lo + n) // 16]))
                 eng = nc.vector if (b == 1 and j >= len(PIECES[b]) - LAST_V) else nc.gpsimd
-                eng.tensor_tensor(res[b][:, xs], picked[b][:, lo : lo + n : 2], picked[b][:, lo + 1 : lo + n : 2], ALU.add)
-                nc.sync.dma_start(out[b * P : (b + 1) * P, xs], res[b][:, xs])
+                eng.tensor_tensor(res[:], picked[:, 0:n:2], picked[:, 1:n:2], ALU.add)
+                nc.sync.dma_start(out[b * P : (b + 1) * P, lo // 2 : (lo + n) // 2], res[:])
                 lo += n

@@ -19,7 +19,7 @@ ALU = mybir.AluOpType
 P = 128
 PACK = 4
 N_MM = 512
-PIECES = [[512,512,512,512],[512,512,512,256,256]]
+PIECES = [[1024,1024],[1024,512,256,256]]
 LAST_V = 1
 
 
@@ -203,10 +203,10 @@ def tile_attend_gmp_sig_ew_kernel(tc, dyT, hE, ew, wm, offs, offs2, out):
         gather(1024, 512, 0, 1)
         sq(0, 512, 1, 2)
         aff(0, 512, 1, 2, 0)
-        gather(0, 512, 1, 0)
+        gather(1024, 512, 1, 1)
         sq(512, 512, 0, 1)
         sq(0, 512, 2, 3)
-        gather(1024, 512, 1, 1)
+        gather(0, 512, 1, 0)
         aff(0, 512, 2, 3, 0)
         aff(512, 512, 0, 1, 0)
         gather(0, 512, 2, 0)
@@ -239,65 +239,79 @@ def tile_attend_gmp_sig_ew_kernel(tc, dyT, hE, ew, wm, offs, offs2, out):
         gather(512, 512, 3, 0)
         weigh(2)
         weigh(3)
-        direct(1024, 256)
+        gather(1536, 512, 0, 1)
         back(2)
         unload(0, 0)
         back(3)
-        weights(0)
+        sq(1536, 512, 0, 2)
         turn(4)
-        gather(1536, 512, 0, 1)
+        gather(1536, 512, 1, 1)
         turn(5)
         unload(1, 0)
+        gather(1536, 512, 2, 1)
         turn(6)
-        direct(1280, 256)
         weigh(4)
-        sq(1536, 512, 0, 2)
+        sq(1536, 512, 2, 4)
         back(4)
-        gather(1536, 512, 1, 1)
+        gather(1536, 512, 3, 1)
         turn(7)
         weigh(5)
-        weights_q()
-        sq(1536, 512, 2, 4)
+        direct(1024, 256)
+        weights(0)
         back(5)
-        gather(1536, 512, 2, 1)
+        direct(1280, 256)
         weigh(6)
-        quantize(1024, 512)
         weigh(7)
-        gather(1536, 512, 3, 1)
-        unload(2, 0)
-        multiply(2, 0)
         back(6)
-        evac(2, 0, 0)
-        quantize(0, 512)
+        unload(2, 0)
+        weights_q()
         back(7)
         direct(1536, 256)
         unload(3, 0)
-        multiply(0, 0)
-        evac(0, 0, 0)
-        quantize(512, 512)
+        quantize(1024, 512)
+        quantize(0, 512)
+        multiply(2, 0)
         direct(1792, 256)
-        multiply(1, 0)
-        evac(1, 0, 0)
+        multiply(0, 0)
+        evac(2, 0, 0)
+        evac(0, 0, 0)
         quantize(1536, 256)
         quantize(1792, 256)
+        quantize(512, 512)
         multiply(3, 0)
+        multiply(1, 0)
+        evac(3, 0, 0)
         multiply(2, 1)
-        evac(3, 0, 1)
+        evac(1, 0, 1)
         multiply(0, 1)
         evac(2, 1, 0)
-        multiply(1, 1)
-        evac(0, 1, 0)
         multiply(3, 1)
-        evac(1, 1, 0)
+        evac(0, 1, 0)
+        multiply(1, 1)
         evac(3, 1, 0)
+        evac(1, 1, 0)
 
+        parts = []
         for b in range(D // P):
             lo = 0
-            for j, n in enumerate(PIECES[b]):
-                picked = keep.tile([P, n], F32, name=f"picked{b}{j}")
-                res = keep.tile([P, n // 2], F32, name=f"res{b}{j}")
-                nc.vector.tensor_copy(picked[:], dm[b][:].indirect(src_list[:, lo // 16 : (lo + n) // 16]))
-                eng = nc.vector if (b == 1 and j >= len(PIECES[b]) - LAST_V) else nc.gpsimd
-                eng.tensor_tensor(res[:], picked[:, 0:n:2], picked[:, 1:n:2], ALU.add)
-                nc.sync.dma_start(out[b * P : (b + 1) * P, lo // 2 : (lo + n) // 2], res[:])
+            for n in PIECES[b]:
+                parts.append((b, lo, n))
                 lo += n
+        picked = {}
+
+        def pick(i):
+            b, lo, n = parts[i]
+            picked[i] = keep.tile([P, n], F32, name=f"picked{i}")
+            nc.vector.tensor_copy(picked[i][:], dm[b][:].indirect(src_list[:, lo // 16 : (lo + n) // 16]))
+
+        def pair_sum(i):
+            b, lo, n = parts[i]
+            res = keep.tile([P, n // 2], F32, name=f"res{i}")
+            nc.vector.tensor_tensor(res[:], picked[i][:, 0:n:2], picked[i][:, 1:n:2], ALU.add)
+            nc.sync.dma_start(out[b * P : (b + 1) * P, lo // 2 : (lo + n) // 2], res[:])
+
+        for i in range(len(parts) + 1):
+            if i < len(parts):
+                pick(i)
+            if i > 0:
+                pair_sum(i - 1)

@@ -17,301 +17,256 @@ ACT = mybir.ActivationFunctionType
 ALU = mybir.AluOpType
 
 P = 128
-PACK = 4
-N_MM = 512
-PIECES = [[1024,1024],[1024,512,256,256]]
-LAST_V = 1
+PLANES = 4
+PER_COLUMN = 16
+CHUNK = 512
+HALF = CHUNK // 2
+BLOCKS = CHUNK // P
+
+TURNED_1, TURNED_2, DIRECT_1, DIRECT_2 = 0, 1, 2, 3
+
+PIECES = ((1024, 1024), (1024, 512, 256, 256))
 
 
 def tile_attend_gmp_sig_ew_kernel(tc, dyT, hE, ew, wm, offs, offs2, out):
     nc = tc.nc
     with ExitStack() as ctx:
         keep = ctx.enter_context(tc.tile_pool(name="keep", bufs=1))
-        ring = ctx.enter_context(tc.tile_pool(name="ring", bufs=4))
-        ps_fwd = ctx.enter_context(tc.psum_pool(name="ps_fwd", bufs=3))
-        ps_back = ctx.enter_context(tc.psum_pool(name="ps_back", bufs=2))
-        ps_mm = ctx.enter_context(tc.psum_pool(name="ps_mm", bufs=3))
+        rounded_pool = ctx.enter_context(tc.tile_pool(name="rounded", bufs=BLOCKS))
+        psum_turn = ctx.enter_context(tc.psum_pool(name="psum_turn", bufs=3))
+        psum_back = ctx.enter_context(tc.psum_pool(name="psum_back", bufs=2))
+        psum_mm = ctx.enter_context(tc.psum_pool(name="psum_mm", bufs=3))
 
-        dst_list = keep.tile([P, E // 16], U16, name="dst_list")
-        src_list = keep.tile([P, E // 16], U16, name="src_list")
-        dy = [keep.tile([P, V], F32, name=f"dy{t}") for t in range(PACK)]
-        CH = 512
-        hs, ews = {}, {}
-        gt = {(c, t): keep.tile([P, CH], F32, name=f"gt{c}{t}") for c in range(2) for t in range(PACK)}
-        gd = {c: keep.tile([P, PACK, CH], F32, name=f"gd{c}") for c in (2, 3)}
-        qd = {c: keep.tile([P, PACK, CH], F32, name=f"qd{c}") for c in (2, 3)}
+        chunks, halves_of_d = range(E // CHUNK), range(D // P)
+        turned_chunks, direct_chunks = (TURNED_1, TURNED_2), (DIRECT_1, DIRECT_2)
+
+        dst_list = keep.tile([P, E // PER_COLUMN], U16, name="dst_list")
+        src_list = keep.tile([P, E // PER_COLUMN], U16, name="src_list")
+        dy = [keep.tile([P, V], F32, name=f"dy{t}") for t in range(PLANES)]
+        h = [keep.tile([P, PLANES, CHUNK], F32, name=f"h{c}") for c in chunks]
+        gathered = [keep.tile([P, PLANES, CHUNK], F32, name=f"gathered{c}") for c in chunks]
+        ew_wide = {c: keep.tile([P, CHUNK], F32, name=f"ew_wide{c}") for c in direct_chunks}
         ew_rows = keep.tile([P, P], F32, name="ew_rows")
         ew_cols = keep.tile([P, E // P], F32, name="ew_cols")
-        ident = keep.tile([P, P], F32, name="ident")
-        w_raw = keep.tile([P, PACK, D], F32, name="w_raw")
-        w_bf = keep.tile([P, D * PACK], BF16, name="w_bf", align_bytes=64)
-        w_codes = keep.tile([P, D], U32, name="w_codes", align_bytes=64)
-        w_scales = keep.tile([P, D], U8, name="w_scales", align_bytes=64)
-        dz_bf = [keep.tile([P, CH * PACK], BF16, name=f"dz_bf{c}", align_bytes=64) for c in range(4)]
-        dz_codes = [keep.tile([P, CH], U32, name=f"dz_codes{c}", align_bytes=64) for c in range(4)]
-        dz_scales = [keep.tile([P, CH], U8, name=f"dz_scales{c}", align_bytes=64) for c in range(4)]
-        dm = [keep.tile([P, E], F32, name=f"dm{b}") for b in range(D // P)]
-        warm = keep.tile([P, 8], F32, name="warm")
-        probe = keep.tile([P, 64], F32, name="probe")
+        identity = keep.tile([P, P], F32, name="identity")
+        w_raw = [keep.tile([P, PLANES, P], F32, name=f"w_raw{b}") for b in halves_of_d]
+        w_bf = [keep.tile([P, P * PLANES], BF16, name=f"w_bf{b}", align_bytes=64) for b in halves_of_d]
+        w_codes = [keep.tile([P, P], U32, name=f"w_codes{b}", align_bytes=64) for b in halves_of_d]
+        w_scales = [keep.tile([P, P], U8, name=f"w_scales{b}", align_bytes=64) for b in halves_of_d]
+        dz_bf = [keep.tile([P, CHUNK * PLANES], BF16, name=f"dz_bf{c}", align_bytes=64) for c in chunks]
+        dz_codes = [keep.tile([P, CHUNK], U32, name=f"dz_codes{c}", align_bytes=64) for c in chunks]
+        dz_scales = [keep.tile([P, CHUNK], U8, name=f"dz_scales{c}", align_bytes=64) for c in chunks]
+        dm = [keep.tile([P, E], F32, name=f"dm{b}") for b in halves_of_d]
 
-        dy_planes = dyT.rearrange("(p t) v -> p t v", t=PACK)
-        h_planes = hE.rearrange("(p t) e -> p t e", t=PACK)
+        dy_planes = dyT.rearrange("(p t) v -> p t v", t=PLANES)
+        h_planes = hE.rearrange("(p t) e -> p t e", t=PLANES)
+        w_planes = wm.rearrange("(p t) d -> p t d", t=PLANES)
 
-        def warm_up():
-            nc.vector.memset(warm[:], 0.0)
-            nc.scalar.activation(out=warm[:, 0:1], in_=warm[:, 1:2], func=ACT.Square, bias=-0.5)
+        def edges(c):
+            return slice(c * CHUNK, (c + 1) * CHUNK)
 
-        def ld_dy(t):
+        def load_h(c, t, count=1):
+            nc.sync.dma_start(h[c][:, t : t + count, :], h_planes[:, t : t + count, edges(c)])
+
+        def load_dy(t):
             nc.sync.dma_start(dy[t][:], dy_planes[:, t, :])
 
-        def ld_h(e0, n, t0, t1):
-            hs[e0, t0] = keep.tile([P, t1 - t0, n], F32, name=f"h{e0}_{t0}")
-            nc.sync.dma_start(hs[e0, t0][:], h_planes[:, t0:t1, e0 : e0 + n])
+        def load_ew(c):
+            nc.sync.dma_start(ew_wide[c][:], ew[:, edges(c)])
 
-        def ld_ew(e0, n):
-            ews[e0] = keep.tile([P, n], F32, name=f"ew{e0}")
-            nc.sync.dma_start(ews[e0][:], ew[:, e0 : e0 + n])
+        def load_w(b):
+            nc.sync.dma_start(w_raw[b][:], w_planes[:, :, b * P : (b + 1) * P])
 
-        def ld_ewr():
-            nc.sync.dma_start(ew_rows[:], ew[0:8, :].rearrange("a (r c) -> (a r) c", c=P))
+        def square(c, t, count=1):
+            x = h[c][:, t : t + count, :]
+            nc.scalar.activation(out=x, in_=x, func=ACT.Square, bias=-0.5)
 
-        def ld_w():
-            nc.sync.dma_start(w_raw[:], wm.rearrange("(p t) d -> p t d", t=PACK))
+        def gather(c, t):
+            entries = dst_list[:, c * CHUNK // PER_COLUMN : (c + 1) * CHUNK // PER_COLUMN]
+            factor = h[c][:, t, :] if c in turned_chunks else ew_wide[c][:]
+            nc.vector.tensor_tensor(gathered[c][:, t, :], dy[t][:].indirect(entries), factor, ALU.mult)
 
-        def ld_l1():
-            nc.sync.dma_start(dst_list[:], offs)
+        def quantize(c, first=0, count=CHUNK):
+            cols = slice(first, first + count)
+            nc.vector.quantize_mx(
+                out=dz_codes[c][:, cols].bitcast(E5M2),
+                scales=dz_scales[c][:, cols],
+                in_=dz_bf[c][:, first * PLANES : (first + count) * PLANES],
+            )
 
-        def ld_l2():
-            nc.sync.dma_start(src_list[:], offs2)
+        turned_bank, rounded, back_bank = {}, {}, {}
 
-        def sq(e0, n, t0, t1):
-            x = hs[e0, t0][:]
-            y = x if e0 < 1024 else qd[e0 // CH][:, t0:t1, :]
-            nc.scalar.activation(out=y, in_=x, func=ACT.Square, bias=-0.5)
+        def less_quarter(c, t):
+            x = h[c][:, t, :]
+            nc.scalar.activation(out=x, in_=x, func=ACT.Copy, scale=1.0, bias=-0.25)
 
-        def aff(e0, n, t0, t1, on_vector):
-            x = hs[e0, t0][:]
-            if on_vector:
-                nc.vector.tensor_scalar(x, x, 1.0, -0.25, ALU.mult, ALU.add)
-            else:
-                nc.scalar.activation(out=x, in_=x, func=ACT.Copy, scale=1.0, bias=-0.25)
+        def turn(c, j):
+            turned_bank[j] = psum_turn.tile([P, PLANES, P], F32, name="turned_bank")
+            for t in range(PLANES):
+                nc.tensor.transpose(turned_bank[j][:, t, :], gathered[c][:, t, j * P : (j + 1) * P], identity[:])
 
-        def gather(e0, n, t, by_ew):
-            lst = dst_list[:, e0 // 16 : (e0 + n) // 16]
-            other = ews[e0][:] if by_ew else hs[e0, t][:, 0, :]
-            nc.vector.tensor_tensor(gd[e0 // CH][:, t, :] if by_ew else gt[e0 // CH, t][:], dy[t][:].indirect(lst), other, ALU.mult)
+        def weigh(c, j):
+            rounded[j] = rounded_pool.tile([P, 2, P, 2], BF16, name="rounded")
+            column = c * BLOCKS + j
+            nc.scalar.activation(
+                out=rounded[j][:],
+                in_=turned_bank[j][:].rearrange("e (u i) p -> e u p i", i=2),
+                func=ACT.Copy,
+                scale=ew_cols[:, column : column + 1],
+            )
 
-        turned, fwd, backs, accs, ew_bank = {}, {}, {}, {}, {}
-
-        def turn(b):
-            fwd[b] = ps_fwd.tile([P, PACK, P], F32, name="fwd")
-            for t in range(PACK):
-                nc.tensor.transpose(fwd[b][:, t, :], gt[b // 4, t][:, (b % 4) * P : (b % 4 + 1) * P], ident[:])
-
-        def weigh(b):
-            turned[b] = ring.tile([P, 2, P, 2], BF16, name="dzt")
-            nc.scalar.activation(out=turned[b][:], in_=fwd[b][:].rearrange("e (u i) p -> e u p i", i=2), func=ACT.Copy,
-                                 scale=ew_cols[:, b : b + 1])
-
-        def back(b):
-            pair, k = divmod(b, 2)
-            if pair not in backs:
-                backs[pair] = ps_back.tile([P, 2, 2 * P], F32, name="back")
-            words = turned[b][:].rearrange("e u p i -> e (u p i)").bitcast(F32)
+        def turn_back(j):
+            pair, place = divmod(j, 2)
+            if place == 0:
+                back_bank[pair] = psum_back.tile([P, 2, HALF], F32, name="back_bank")
+            words = rounded[j][:].rearrange("e u p i -> e (u p i)").bitcast(F32)
             for u in range(2):
-                nc.tensor.transpose(backs[pair][:, u, k * P : (k + 1) * P], words[:, u * P : (u + 1) * P], ident[:])
+                nc.tensor.transpose(
+                    back_bank[pair][:, u, place * P : (place + 1) * P], words[:, u * P : (u + 1) * P], identity[:]
+                )
 
-        def unload(pair, on_vector):
-            dst = dz_bf[pair // 2][:, (pair % 2) * 2 * P * PACK : (pair % 2 + 1) * 2 * P * PACK].bitcast(F32).rearrange("p (e u) -> p e u", u=2)
-            if on_vector:
-                nc.vector.tensor_copy(dst, backs[pair][:].rearrange("p u e -> p e u"))
-            else:
-                nc.scalar.copy(dst, backs[pair][:].rearrange("p u e -> p e u"))
+        def unload(c, pair):
+            words = dz_bf[c][:, pair * HALF * PLANES : (pair + 1) * HALF * PLANES].bitcast(F32)
+            nc.scalar.copy(words.rearrange("p (e u) -> p e u", u=2), back_bank[pair][:].rearrange("p u e -> p e u"))
 
-        def direct(e0, n):
-            c, e0 = divmod(e0, CH)
-            dst = dz_bf[c][:, e0 * PACK : (e0 + n) * PACK].rearrange("p (e t) -> p e t", t=PACK)
+        def turned_road(c, fillers):
+            for j in range(BLOCKS - 1):
+                turn(c, j)
+            weigh(c, 0)
+            turn_back(0)
+            turn(c, BLOCKS - 1)
+            fillers[0]()
+            weigh(c, 1)
+            turn_back(1)
+            fillers[1]()
+            for j in (2, 3):
+                weigh(c, j)
+                turn_back(j)
+            unload(c, 0)
+            for filler in fillers[2:]:
+                filler()
+            unload(c, 1)
+
+        def finish_direct(c, first):
+            cols = slice(first, first + HALF)
             nc.vector.scalar_tensor_tensor(
-                dst, qd[c][:, :, e0 : e0 + n].rearrange("p t e -> p e t"), 0.25,
-                gd[c][:, :, e0 : e0 + n].rearrange("p t e -> p e t"), ALU.subtract, ALU.mult)
+                dz_bf[c][:, first * PLANES : (first + HALF) * PLANES].rearrange("p (e t) -> p e t", t=PLANES),
+                h[c][:, :, cols].rearrange("p t e -> p e t"),
+                0.25,
+                gathered[c][:, :, cols].rearrange("p t e -> p e t"),
+                ALU.subtract,
+                ALU.mult,
+            )
 
-        def quantize(e0, n):
-            c, e0 = divmod(e0, CH)
-            nc.vector.quantize_mx(out=dz_codes[c][:, e0 : e0 + n].bitcast(E5M2), scales=dz_scales[c][:, e0 : e0 + n],
-                                  in_=dz_bf[c][:, e0 * PACK : (e0 + n) * PACK])
+        def round_w(b):
+            nc.scalar.copy(w_bf[b][:].rearrange("p (d t) -> p d t", t=PLANES), w_raw[b][:].rearrange("p t d -> p d t"))
 
-        def multiply(c, b):
-            cols = slice(c * N_MM, (c + 1) * N_MM)
-            accs[c, b] = ps_mm.tile([P, N_MM], F32, name="acc")
-            nc.tensor.matmul_mx(out=accs[c, b][:], lhsT=w_codes[:, b * P : (b + 1) * P].bitcast(E4M3),
-                                lhsT_scale=w_scales[:, b * P : (b + 1) * P],
-                                rhs=dz_codes[c][:].bitcast(E5M2), rhs_scale=dz_scales[c][:],
-                                start=True, stop=True)
+        def quantize_w(b):
+            nc.vector.quantize_mx(out=w_codes[b][:].bitcast(E4M3), scales=w_scales[b][:], in_=w_bf[b][:])
 
-        def evac(c, b, on_vector):
-            cols = slice(c * N_MM, (c + 1) * N_MM)
-            if on_vector:
-                nc.vector.tensor_scalar(dm[b][:, cols], accs[c, b][:], -1.0, None, ALU.mult)
+        def multiply(c, b, out_on_vector=False):
+            sums = psum_mm.tile([P, CHUNK], F32, name="sums")
+            nc.tensor.matmul_mx(
+                out=sums[:],
+                lhsT=w_codes[b][:].bitcast(E4M3),
+                lhsT_scale=w_scales[b][:],
+                rhs=dz_codes[c][:].bitcast(E5M2),
+                rhs_scale=dz_scales[c][:],
+                start=True,
+                stop=True,
+            )
+            if out_on_vector:
+                nc.vector.tensor_scalar(dm[b][:, edges(c)], sums[:], -1.0, None, ALU.mult)
             else:
-                nc.scalar.activation(out=dm[b][:, cols], in_=accs[c, b][:], func=ACT.Copy, scale=-1.0)
+                nc.scalar.activation(out=dm[b][:, edges(c)], in_=sums[:], func=ACT.Copy, scale=-1.0)
 
-        def weights(on_vector):
-            src = w_raw[:].rearrange("p t d -> p d t")
-            dst = w_bf[:].rearrange("p (d t) -> p d t", t=PACK)
-            if on_vector:
-                nc.vector.tensor_copy(dst, src)
-            else:
-                nc.scalar.copy(dst, src)
+        load_h(TURNED_1, 0)
+        load_dy(0)
+        nc.sync.dma_start(dst_list[:], offs)
+        load_ew(DIRECT_1)
+        for t in range(1, PLANES):
+            load_h(TURNED_1, t)
+            load_dy(t)
+            if t < PLANES - 1:
+                load_h(TURNED_2, t - 1)
+        nc.sync.dma_start(ew_rows[:], ew[0 : P * P // E, :].rearrange("a (r c) -> (a r) c", c=P))
+        load_h(TURNED_2, 2)
+        load_h(TURNED_2, 3)
+        load_h(DIRECT_1, 0, 2)
+        load_h(DIRECT_1, 2, 2)
+        load_ew(DIRECT_2)
+        load_w(0)
+        load_h(DIRECT_2, 0, 2)
+        load_h(DIRECT_2, 2, 2)
+        load_w(1)
+        nc.sync.dma_start(src_list[:], offs2)
 
-        def weights_q():
-            nc.vector.quantize_mx(out=w_codes[:].bitcast(E4M3), scales=w_scales[:], in_=w_bf[:])
+        square(TURNED_1, 0)
+        nc.vector.tensor_scalar(h[TURNED_1][:, 0, :], h[TURNED_1][:, 0, :], 1.0, -0.25, ALU.mult, ALU.add)
+        gather(TURNED_1, 0)
+        gather(DIRECT_1, 0)
+        square(TURNED_1, 1)
+        less_quarter(TURNED_1, 1)
+        for t in (1, 2):
+            gather(DIRECT_1, t)
+            gather(TURNED_1, t)
+            if t == 1:
+                square(TURNED_2, 0)
+                square(TURNED_1, 2)
+                less_quarter(TURNED_1, 2)
+        less_quarter(TURNED_2, 0)
+        square(TURNED_1, 3)
+        square(TURNED_2, 1)
+        less_quarter(TURNED_1, 3)
+        less_quarter(TURNED_2, 1)
+        gather(TURNED_1, 3)
+        gather(DIRECT_1, 3)
 
-        def ew_turn():
-            make_identity(nc, ident[:])
-            ew_bank[0] = ps_mm.tile([P, N_MM], F32, name="acc")
-            nc.tensor.transpose(ew_bank[0][:, 0:P], ew_rows[:], ident[:])
+        make_identity(nc, identity[:])
+        ew_bank = psum_mm.tile([P, CHUNK], F32, name="sums")
+        nc.tensor.transpose(ew_bank[:, 0:P], ew_rows[:], identity[:])
+        nc.scalar.copy(ew_cols[:], ew_bank[:, 0 : E // P])
 
-        def ew_copy():
-            nc.scalar.copy(ew_cols[:], ew_bank[0][:, 0 : E // P])
+        for t in (2, 3):
+            square(TURNED_2, t)
+        for t in (2, 3):
+            less_quarter(TURNED_2, t)
+        for c in (TURNED_2, DIRECT_2):
+            for t in range(PLANES):
+                gather(c, t)
 
-        warm_up()
-        ld_h(0, 512, 0, 1)
-        ld_dy(0)
-        ld_l1()
-        ld_ew(1024, 512)
-        ld_h(0, 512, 1, 2)
-        ld_dy(1)
-        ld_h(512, 512, 0, 1)
-        ld_h(0, 512, 2, 3)
-        ld_dy(2)
-        ld_h(512, 512, 1, 2)
-        ld_h(0, 512, 3, 4)
-        ld_dy(3)
-        ld_ewr()
-        ld_h(512, 512, 2, 3)
-        ld_h(512, 512, 3, 4)
-        ld_h(1024, 512, 0, 2)
-        ld_h(1024, 512, 2, 4)
-        ld_ew(1536, 512)
-        ld_w()
-        ld_h(1536, 512, 0, 2)
-        ld_h(1536, 512, 2, 4)
-        ld_l2()
-        sq(0, 512, 0, 1)
-        aff(0, 512, 0, 1, 1)
-        gather(0, 512, 0, 0)
-        gather(1024, 512, 0, 1)
-        sq(0, 512, 1, 2)
-        aff(0, 512, 1, 2, 0)
-        gather(1024, 512, 1, 1)
-        sq(512, 512, 0, 1)
-        sq(0, 512, 2, 3)
-        gather(0, 512, 1, 0)
-        aff(0, 512, 2, 3, 0)
-        aff(512, 512, 0, 1, 0)
-        gather(0, 512, 2, 0)
-        sq(512, 512, 1, 2)
-        sq(0, 512, 3, 4)
-        gather(1024, 512, 2, 1)
-        aff(0, 512, 3, 4, 0)
-        ew_turn()
-        aff(512, 512, 1, 2, 0)
-        gather(0, 512, 3, 0)
-        ew_copy()
-        sq(512, 512, 2, 3)
-        sq(512, 512, 3, 4)
-        gather(1024, 512, 3, 1)
-        turn(0)
-        aff(512, 512, 2, 3, 0)
-        aff(512, 512, 3, 4, 0)
-        turn(1)
-        gather(512, 512, 0, 0)
-        weigh(0)
-        turn(2)
-        sq(1024, 512, 0, 2)
-        gather(512, 512, 1, 0)
-        back(0)
-        turn(3)
-        weigh(1)
-        gather(512, 512, 2, 0)
-        sq(1024, 512, 2, 4)
-        back(1)
-        gather(512, 512, 3, 0)
-        weigh(2)
-        weigh(3)
-        gather(1536, 512, 0, 1)
-        back(2)
-        unload(0, 0)
-        back(3)
-        sq(1536, 512, 0, 2)
-        turn(4)
-        gather(1536, 512, 1, 1)
-        turn(5)
-        unload(1, 0)
-        gather(1536, 512, 2, 1)
-        turn(6)
-        weigh(4)
-        sq(1536, 512, 2, 4)
-        back(4)
-        gather(1536, 512, 3, 1)
-        turn(7)
-        weigh(5)
-        direct(1024, 256)
-        weights(0)
-        back(5)
-        direct(1280, 256)
-        weigh(6)
-        weigh(7)
-        back(6)
-        unload(2, 0)
-        weights_q()
-        back(7)
-        direct(1536, 256)
-        unload(3, 0)
-        quantize(1024, 512)
-        quantize(0, 512)
-        multiply(2, 0)
-        direct(1792, 256)
-        multiply(0, 0)
-        evac(2, 0, 0)
-        evac(0, 0, 0)
-        quantize(1536, 256)
-        quantize(1792, 256)
-        quantize(512, 512)
-        multiply(3, 0)
-        multiply(1, 0)
-        evac(3, 0, 0)
-        multiply(2, 1)
-        evac(1, 0, 1)
-        multiply(0, 1)
-        evac(2, 1, 0)
-        multiply(3, 1)
-        evac(0, 1, 0)
-        multiply(1, 1)
-        evac(3, 1, 0)
-        evac(1, 1, 0)
+        turned_road(
+            TURNED_1, [lambda: square(DIRECT_1, 0, 2), lambda: square(DIRECT_1, 2, 2), lambda: square(DIRECT_2, 0, 2)]
+        )
+        turned_road(TURNED_2, [lambda: square(DIRECT_2, 2, 2), lambda: round_w(0)])
+        round_w(1)
 
-        parts = []
-        for b in range(D // P):
-            lo = 0
-            for n in PIECES[b]:
-                parts.append((b, lo, n))
-                lo += n
-        picked = {}
+        finish_direct(DIRECT_1, 0)
+        finish_direct(DIRECT_1, HALF)
+        quantize_w(0)
+        finish_direct(DIRECT_2, 0)
+        quantize(DIRECT_1)
+        quantize(TURNED_1)
+        finish_direct(DIRECT_2, HALF)
+        quantize(DIRECT_2, 0, HALF)
+        quantize(DIRECT_2, HALF, HALF)
+        quantize(TURNED_2)
+        quantize_w(1)
 
-        def pick(i):
-            b, lo, n = parts[i]
-            picked[i] = keep.tile([P, n], F32, name=f"picked{i}")
-            nc.vector.tensor_copy(picked[i][:], dm[b][:].indirect(src_list[:, lo // 16 : (lo + n) // 16]))
+        order = (DIRECT_1, TURNED_1, DIRECT_2, TURNED_2)
+        for b in halves_of_d:
+            for c in order:
+                multiply(c, b, out_on_vector=(b == 0 and c == order[-1]))
 
-        def pair_sum(i):
-            b, lo, n = parts[i]
-            res = keep.tile([P, n // 2], F32, name=f"res{i}")
-            nc.vector.tensor_tensor(res[:], picked[i][:, 0:n:2], picked[i][:, 1:n:2], ALU.add)
-            nc.sync.dma_start(out[b * P : (b + 1) * P, lo // 2 : (lo + n) // 2], res[:])
-
-        for i in range(len(parts) + 1):
-            if i < len(parts):
-                pick(i)
-            if i > 0:
-                pair_sum(i - 1)
+        for b in halves_of_d:
+            first = 0
+            for count in PIECES[b]:
+                picked = keep.tile([P, count], F32, name=f"picked{b}_{first}")
+                summed = keep.tile([P, count // 2], F32, name=f"summed{b}_{first}")
+                entries = src_list[:, first // PER_COLUMN : (first + count) // PER_COLUMN]
+                nc.vector.tensor_copy(picked[:], dm[b][:].indirect(entries))
+                last = b == halves_of_d[-1] and first + count == E
+                adder = nc.vector if last else nc.gpsimd
+                adder.tensor_tensor(summed[:], picked[:, 0:count:2], picked[:, 1:count:2], ALU.add)
+                nc.sync.dma_start(out[b * P : (b + 1) * P, first // 2 : (first + count) // 2], summed[:])
+                first += count

from contextlib import ExitStack

import concourse.mybir as mybir
from concourse.masks import make_identity

V, E, D, DV = 1024, 2048, 256, 512
FLOPS = 2 * DV * D * E

F32 = mybir.dt.float32
BF16 = mybir.dt.bfloat16
U32 = mybir.dt.uint32
U16 = mybir.dt.uint16
U8 = mybir.dt.uint8
E4M3 = mybir.dt.float8_e4m3fn_x4
E5M2 = mybir.dt.float8_e5m2_x4
ACT = mybir.ActivationFunctionType
ALU = mybir.AluOpType

P = 128
PLANES = 4
PER_COLUMN = 16
CHUNK = 512
HALF = CHUNK // 2
BLOCKS = CHUNK // P

TURNED_1, TURNED_2, DIRECT_1, DIRECT_2 = 0, 1, 2, 3

PIECES = ((1024, 1024), (1024, 512, 256, 256))


def tile_attend_gmp_sig_ew_kernel(tc, dyT, hE, ew, wm, offs, offs2, out):
    nc = tc.nc
    with ExitStack() as ctx:
        keep = ctx.enter_context(tc.tile_pool(name="keep", bufs=1))
        rounded_pool = ctx.enter_context(tc.tile_pool(name="rounded", bufs=BLOCKS))
        psum_turn = ctx.enter_context(tc.psum_pool(name="psum_turn", bufs=3))
        psum_back = ctx.enter_context(tc.psum_pool(name="psum_back", bufs=2))
        psum_mm = ctx.enter_context(tc.psum_pool(name="psum_mm", bufs=3))

        chunks, halves_of_d = range(E // CHUNK), range(D // P)
        turned_chunks, direct_chunks = (TURNED_1, TURNED_2), (DIRECT_1, DIRECT_2)

        dst_list = keep.tile([P, E // PER_COLUMN], U16, name="dst_list")
        src_list = keep.tile([P, E // PER_COLUMN], U16, name="src_list")
        dy = [keep.tile([P, V], F32, name=f"dy{t}") for t in range(PLANES)]
        h = [keep.tile([P, PLANES, CHUNK], F32, name=f"h{c}") for c in chunks]
        gathered = [keep.tile([P, PLANES, CHUNK], F32, name=f"gathered{c}") for c in chunks]
        ew_wide = {c: keep.tile([P, CHUNK], F32, name=f"ew_wide{c}") for c in direct_chunks}
        ew_rows = keep.tile([P, P], F32, name="ew_rows")
        ew_cols = keep.tile([P, E // P], F32, name="ew_cols")
        identity = keep.tile([P, P], F32, name="identity")
        w_raw = [keep.tile([P, PLANES, P], F32, name=f"w_raw{b}") for b in halves_of_d]
        w_bf = [keep.tile([P, P * PLANES], BF16, name=f"w_bf{b}", align_bytes=64) for b in halves_of_d]
        w_codes = [keep.tile([P, P], U32, name=f"w_codes{b}", align_bytes=64) for b in halves_of_d]
        w_scales = [keep.tile([P, P], U8, name=f"w_scales{b}", align_bytes=64) for b in halves_of_d]
        dz_bf = [keep.tile([P, CHUNK * PLANES], BF16, name=f"dz_bf{c}", align_bytes=64) for c in chunks]
        dz_codes = [keep.tile([P, CHUNK], U32, name=f"dz_codes{c}", align_bytes=64) for c in chunks]
        dz_scales = [keep.tile([P, CHUNK], U8, name=f"dz_scales{c}", align_bytes=64) for c in chunks]
        dm = [keep.tile([P, E], F32, name=f"dm{b}") for b in halves_of_d]

        dy_planes = dyT.rearrange("(p t) v -> p t v", t=PLANES)
        h_planes = hE.rearrange("(p t) e -> p t e", t=PLANES)
        w_planes = wm.rearrange("(p t) d -> p t d", t=PLANES)

        def edges(c):
            return slice(c * CHUNK, (c + 1) * CHUNK)

        def load_h(c, t, count=1):
            nc.sync.dma_start(h[c][:, t : t + count, :], h_planes[:, t : t + count, edges(c)])

        def load_dy(t):
            nc.sync.dma_start(dy[t][:], dy_planes[:, t, :])

        def load_ew(c):
            nc.sync.dma_start(ew_wide[c][:], ew[:, edges(c)])

        def load_w(b):
            nc.sync.dma_start(w_raw[b][:], w_planes[:, :, b * P : (b + 1) * P])

        def square(c, t, count=1):
            x = h[c][:, t : t + count, :]
            nc.scalar.activation(out=x, in_=x, func=ACT.Square, bias=-0.5)

        def gather(c, t):
            entries = dst_list[:, c * CHUNK // PER_COLUMN : (c + 1) * CHUNK // PER_COLUMN]
            factor = h[c][:, t, :] if c in turned_chunks else ew_wide[c][:]
            nc.vector.tensor_tensor(gathered[c][:, t, :], dy[t][:].indirect(entries), factor, ALU.mult)

        def quantize(c, first=0, count=CHUNK):
            cols = slice(first, first + count)
            nc.vector.quantize_mx(
                out=dz_codes[c][:, cols].bitcast(E5M2),
                scales=dz_scales[c][:, cols],
                in_=dz_bf[c][:, first * PLANES : (first + count) * PLANES],
            )

        turned_bank, rounded, back_bank = {}, {}, {}

        def less_quarter(c, t):
            x = h[c][:, t, :]
            nc.scalar.activation(out=x, in_=x, func=ACT.Copy, scale=1.0, bias=-0.25)

        def turn(c, j):
            turned_bank[j] = psum_turn.tile([P, PLANES, P], F32, name="turned_bank")
            for t in range(PLANES):
                nc.tensor.transpose(turned_bank[j][:, t, :], gathered[c][:, t, j * P : (j + 1) * P], identity[:])

        def weigh(c, j):
            rounded[j] = rounded_pool.tile([P, 2, P, 2], BF16, name="rounded")
            column = c * BLOCKS + j
            nc.scalar.activation(
                out=rounded[j][:],
                in_=turned_bank[j][:].rearrange("e (u i) p -> e u p i", i=2),
                func=ACT.Copy,
                scale=ew_cols[:, column : column + 1],
            )

        def turn_back(j):
            pair, place = divmod(j, 2)
            if place == 0:
                back_bank[pair] = psum_back.tile([P, 2, HALF], F32, name="back_bank")
            words = rounded[j][:].rearrange("e u p i -> e (u p i)").bitcast(F32)
            for u in range(2):
                nc.tensor.transpose(
                    back_bank[pair][:, u, place * P : (place + 1) * P], words[:, u * P : (u + 1) * P], identity[:]
                )

        def unload(c, pair):
            words = dz_bf[c][:, pair * HALF * PLANES : (pair + 1) * HALF * PLANES].bitcast(F32)
            nc.scalar.copy(words.rearrange("p (e u) -> p e u", u=2), back_bank[pair][:].rearrange("p u e -> p e u"))

        def turned_road(c, fillers):
            for j in range(BLOCKS - 1):
                turn(c, j)
            weigh(c, 0)
            turn_back(0)
            turn(c, BLOCKS - 1)
            fillers[0]()
            weigh(c, 1)
            turn_back(1)
            fillers[1]()
            for j in (2, 3):
                weigh(c, j)
                turn_back(j)
            unload(c, 0)
            for filler in fillers[2:]:
                filler()
            unload(c, 1)

        def finish_direct(c, first):
            cols = slice(first, first + HALF)
            nc.vector.scalar_tensor_tensor(
                dz_bf[c][:, first * PLANES : (first + HALF) * PLANES].rearrange("p (e t) -> p e t", t=PLANES),
                h[c][:, :, cols].rearrange("p t e -> p e t"),
                0.25,
                gathered[c][:, :, cols].rearrange("p t e -> p e t"),
                ALU.subtract,
                ALU.mult,
            )

        def round_w(b):
            nc.scalar.copy(w_bf[b][:].rearrange("p (d t) -> p d t", t=PLANES), w_raw[b][:].rearrange("p t d -> p d t"))

        def quantize_w(b):
            nc.vector.quantize_mx(out=w_codes[b][:].bitcast(E4M3), scales=w_scales[b][:], in_=w_bf[b][:])

        def multiply(c, b, out_on_vector=False):
            sums = psum_mm.tile([P, CHUNK], F32, name="sums")
            nc.tensor.matmul_mx(
                out=sums[:],
                lhsT=w_codes[b][:].bitcast(E4M3),
                lhsT_scale=w_scales[b][:],
                rhs=dz_codes[c][:].bitcast(E5M2),
                rhs_scale=dz_scales[c][:],
                start=True,
                stop=True,
            )
            if out_on_vector:
                nc.vector.tensor_scalar(dm[b][:, edges(c)], sums[:], -1.0, None, ALU.mult)
            else:
                nc.scalar.activation(out=dm[b][:, edges(c)], in_=sums[:], func=ACT.Copy, scale=-1.0)

        load_h(TURNED_1, 0)
        load_dy(0)
        nc.sync.dma_start(dst_list[:], offs)
        load_ew(DIRECT_1)
        for t in range(1, PLANES):
            load_h(TURNED_1, t)
            load_dy(t)
            if t < PLANES - 1:
                load_h(TURNED_2, t - 1)
        nc.sync.dma_start(ew_rows[:], ew[0 : P * P // E, :].rearrange("a (r c) -> (a r) c", c=P))
        load_h(TURNED_2, 2)
        load_h(TURNED_2, 3)
        load_h(DIRECT_1, 0, 2)
        load_h(DIRECT_1, 2, 2)
        load_ew(DIRECT_2)
        load_w(0)
        load_h(DIRECT_2, 0, 2)
        load_h(DIRECT_2, 2, 2)
        load_w(1)
        nc.sync.dma_start(src_list[:], offs2)

        square(TURNED_1, 0)
        nc.vector.tensor_scalar(h[TURNED_1][:, 0, :], h[TURNED_1][:, 0, :], 1.0, -0.25, ALU.mult, ALU.add)
        gather(TURNED_1, 0)
        gather(DIRECT_1, 0)
        square(TURNED_1, 1)
        less_quarter(TURNED_1, 1)
        for t in (1, 2):
            gather(DIRECT_1, t)
            gather(TURNED_1, t)
            if t == 1:
                square(TURNED_2, 0)
                square(TURNED_1, 2)
                less_quarter(TURNED_1, 2)
        less_quarter(TURNED_2, 0)
        square(TURNED_1, 3)
        square(TURNED_2, 1)
        less_quarter(TURNED_1, 3)
        less_quarter(TURNED_2, 1)
        gather(TURNED_1, 3)
        gather(DIRECT_1, 3)

        make_identity(nc, identity[:])
        ew_bank = psum_mm.tile([P, CHUNK], F32, name="sums")
        nc.tensor.transpose(ew_bank[:, 0:P], ew_rows[:], identity[:])
        nc.scalar.copy(ew_cols[:], ew_bank[:, 0 : E // P])

        for t in (2, 3):
            square(TURNED_2, t)
        for t in (2, 3):
            less_quarter(TURNED_2, t)
        for c in (TURNED_2, DIRECT_2):
            for t in range(PLANES):
                gather(c, t)

        turned_road(
            TURNED_1, [lambda: square(DIRECT_1, 0, 2), lambda: square(DIRECT_1, 2, 2), lambda: square(DIRECT_2, 0, 2)]
        )
        turned_road(TURNED_2, [lambda: square(DIRECT_2, 2, 2), lambda: round_w(0)])
        round_w(1)

        finish_direct(DIRECT_1, 0)
        finish_direct(DIRECT_1, HALF)
        quantize_w(0)
        finish_direct(DIRECT_2, 0)
        quantize(DIRECT_1)
        quantize(TURNED_1)
        finish_direct(DIRECT_2, HALF)
        quantize(DIRECT_2, 0, HALF)
        quantize(DIRECT_2, HALF, HALF)
        quantize(TURNED_2)
        quantize_w(1)

        order = (DIRECT_1, TURNED_1, DIRECT_2, TURNED_2)
        for b in halves_of_d:
            for c in order:
                multiply(c, b, out_on_vector=(b == 0 and c == order[-1]))

        for b in halves_of_d:
            first = 0
            for count in PIECES[b]:
                picked = keep.tile([P, count], F32, name=f"picked{b}_{first}")
                summed = keep.tile([P, count // 2], F32, name=f"summed{b}_{first}")
                entries = src_list[:, first // PER_COLUMN : (first + count) // PER_COLUMN]
                nc.vector.tensor_copy(picked[:], dm[b][:].indirect(entries))
                last = b == halves_of_d[-1] and first + count == E
                adder = nc.vector if last else nc.gpsimd
                adder.tensor_tensor(summed[:], picked[:, 0:count:2], picked[:, 1:count:2], ALU.add)
                nc.sync.dma_start(out[b * P : (b + 1) * P, first // 2 : (first + count) // 2], summed[:])
                first += count
